import numpy as np
import ml_dtypes


def mxq(x, axis, fmt="e4m3"):
    dtype, down = {"e4m3": (ml_dtypes.float8_e4m3fn, 7), "e5m2": (ml_dtypes.float8_e5m2, 14)}[fmt]
    v = np.moveaxis(np.asarray(x, np.float32).astype(ml_dtypes.bfloat16).astype(np.float64), axis, -1)
    blocks = v.reshape(v.shape[:-1] + (-1, 32))
    amax = np.abs(blocks).max(-1, keepdims=True)
    byte = np.maximum(np.where(amax > 0, np.frexp(amax)[1] - 1 + 127, 0) - down, 1)
    scale = np.exp2(byte - 127.0)
    codes = (blocks / scale).astype(np.float32).astype(dtype).astype(np.float64)
    return np.moveaxis((codes * scale).reshape(v.shape), -1, axis)


WIDE = False


def mx_kscale(k):
    if not WIDE:
        return np.ones(k)
    levels = np.array([10, -10, 5, -5, 0])
    if k % 512:
        return np.exp2(np.random.permutation(np.resize(levels, k // 32))).repeat(32)
    a = np.empty((k // 512, 16))
    for p in range(k // 512):
        a[p, :8] = np.random.permutation(np.resize(levels, 8))
        for g in range(8):
            far = levels[np.abs(levels - a[p, g]) >= 10]
            a[p, g + 8] = far[np.random.randint(len(far))]
    return np.exp2(a.ravel()).repeat(32)


def f64(x):
    return np.asarray(x).astype(np.float64)


def striped(idx):
    return np.tile(idx.reshape(-1, 16).T, (8, 1)).astype(np.uint16)


def unstriped(offs):
    return offs[:16].T.reshape(-1).astype(np.int64)


def pack_weight(w):
    k, n = w.shape
    w = f64(np.asarray(w, np.float32).astype(ml_dtypes.bfloat16)).reshape(k // 32, 32, n)
    amax = np.abs(w).max(1)
    byte = np.clip(np.where(amax > 0, np.frexp(amax)[1] - 1 + 127 - 7, 1), 1, 254)
    scaled = (w * np.exp2(127.0 - byte)[:, None, :]).reshape(k, n).astype(np.float32)
    words = np.ascontiguousarray(scaled.reshape(k // 512, 128, 4, n).transpose(0, 1, 3, 2)).astype(ml_dtypes.float8_e4m3fn).view(np.uint8)
    return words, np.ascontiguousarray(byte.astype(np.uint8).reshape(k // 512, 16, n))


def unpack_weight(words, scales):
    g, p, n, _ = words.shape
    vals = np.ascontiguousarray(words).view(ml_dtypes.float8_e4m3fn).astype(np.float64) * np.repeat(np.exp2(scales.astype(np.float64) - 127.0), 8, axis=1)[..., None]
    return vals.transpose(0, 1, 3, 2).reshape(g * 512, n)


K, T, S, V, R, W = 512, 2048, 512, 512, 256, 1024


def setup_inputs():
    n = np.random.standard_normal
    s = mx_kscale(K)[:, None]
    packed_xT = pack_weight(n((K, T)) * s)
    packed_eT = pack_weight(n((K, W)) * s)
    return {
        "x_words": packed_xT[0],
        "x_scales": packed_xT[1],
        "hT": (n((K, V)) / np.sqrt(K) / s).astype(np.float32),
        "e_words": packed_eT[0],
        "e_scales": packed_eT[1],
        "offs": striped(np.random.permutation(T)[:S]),
        "past": striped(np.random.permutation(W)[:R]),
        "word": striped(np.random.permutation(S)[:R]),
    }


def reference(x_words, x_scales, hT, e_words, e_scales, offs, past, word):
    hTq = mxq(f64(hT), 0, "e4m3")
    xq = unpack_weight(x_words, x_scales)[:, unstriped(offs)]
    y = hTq.T @ xq
    ex = np.exp(y - y.max(axis=1, keepdims=True))
    p = ex / ex.sum(axis=1, keepdims=True)
    e_past = unpack_weight(e_words, e_scales)[:, unstriped(past)]
    z = 0.7 * (hTq.T @ e_past)
    ex2 = np.exp(z - z.max(axis=1, keepdims=True))
    qq = ex2 / ex2.sum(axis=1, keepdims=True)
    cp = np.zeros((K, S))
    cp[:, unstriped(word)] = 0.25 * qq
    return 0.75 * p + cp

@@ -1,0 +1,178 @@
+from contextlib import ExitStack
+
+import concourse.mybir as mybir
+
+K, T, S, V, R, W = 512, 2048, 512, 512, 256, 1024
+FLOPS = 2 * K * V * (S + R)
+
+F32 = mybir.dt.float32
+BF16 = mybir.dt.bfloat16
+I32 = mybir.dt.int32
+U32 = mybir.dt.uint32
+U16 = mybir.dt.uint16
+U8 = mybir.dt.uint8
+FP8X4 = mybir.dt.float8_e4m3fn_x4
+ALU = mybir.AluOpType
+ACT = mybir.ActivationFunctionType
+AXIS_X = mybir.AxisListType.X
+
+P = 128
+PACK = 4
+BLOCKS = V // P
+PAIRS = BLOCKS // 2
+
+
+def tile_picked_ycache_mix_p_kernel(tc, x_words, x_scales, hT, e_words, e_scales, offs, past, word, out):
+    nc = tc.nc
+    with ExitStack() as ctx:
+        keep = ctx.enter_context(tc.tile_pool(name="keep", bufs=1))
+        psum = ctx.enter_context(tc.psum_pool(name="psum", bufs=1))
+
+        offs_t = keep.tile([P, S // 16], U16, name="offs_t")
+        past_t = keep.tile([P, R // 16], U16, name="past_t")
+        word_t = keep.tile([P, R // 16], U16, name="word_t")
+        xw = keep.tile([P, T], I32, name="xw")
+        ew = keep.tile([P, W], I32, name="ew")
+        xs = keep.tile([P, T], U8, name="xs")
+        es = keep.tile([P, W], U8, name="es")
+        h_raw = [keep.tile([P, PACK, 2 * P], F32, name=f"h_raw{i}") for i in range(PAIRS)]
+        cp = [keep.tile([P, S], F32, name=f"cp{b}") for b in range(BLOCKS)]
+        warm = keep.tile([P, 1], F32, name="warm")
+        warm_out = keep.tile([P, 1], F32, name="warm_out")
+
+        nc.gpsimd.memset(es[:].bitcast(I32), 0)
+        nc.vector.memset(warm[:], 0.0)
+        nc.vector.memset(xs[:].bitcast(I32), 0)
+        nc.scalar.activation(warm_out[:], warm[:], ACT.Exp)
+        for b in range(BLOCKS):
+            nc.vector.memset(cp[b][:], 0.0)
+
+        def load_scales(tile, scales):
+            rows = scales[0].rearrange("(q r) n -> r q n", r=4)
+            for r in range(4):
+                nc.sync.dma_start(tile[r:P:32, :].bitcast(I32), rows[r].bitcast(I32))
+
+        h_view = hT.rearrange("(p j) t -> p j t", j=PACK)
+        nc.sync.dma_start(past_t[:], past)
+        nc.sync.dma_start(offs_t[:], offs)
+        nc.sync.dma_start(ew[:], e_words[0].rearrange("p n t -> p (n t)").bitcast(I32))
+        load_scales(es, e_scales)
+        nc.sync.dma_start(h_raw[0][:], h_view[:, :, 0 : 2 * P])
+        load_scales(xs, x_scales)
+        nc.sync.dma_start(xw[:], x_words[0].rearrange("p n t -> p (n t)").bitcast(I32))
+        nc.sync.dma_start(h_raw[1][:], h_view[:, :, 2 * P : 4 * P])
+        nc.sync.dma_start(word_t[:], word)
+
+        eg_w = keep.tile([P, R], U32, name="eg_w", align_bytes=64)
+        eg_s = keep.tile([P, R], U8, name="eg_s", align_bytes=64)
+        xg_w = keep.tile([P, S], U32, name="xg_w", align_bytes=64)
+        xg_s = keep.tile([P, S], U8, name="xg_s", align_bytes=64)
+        h_bf = [keep.tile([P, P, PACK], BF16, name=f"h_bf{b}", align_bytes=64) for b in range(BLOCKS)]
+        h_w = [keep.tile([P, P], U32, name=f"h_w{b}", align_bytes=64) for b in range(BLOCKS)]
+        h_s = [keep.tile([P, P], U8, name=f"h_s{b}", align_bytes=64) for b in range(BLOCKS)]
+        z_ps = [psum.tile([P, 2, R], F32, name=f"z_ps{i}") for i in range(PAIRS)]
+        y_ps = [psum.tile([P, S], F32, name=f"y_ps{b}") for b in range(BLOCKS)]
+        z_negmax = [keep.tile([P, 2], F32, name=f"z_negmax{i}") for i in range(PAIRS)]
+        z_bias = [keep.tile([P, 2], F32, name=f"z_bias{i}") for i in range(PAIRS)]
+        y_negmax = [keep.tile([P, 1], F32, name=f"y_negmax{b}") for b in range(BLOCKS)]
+        sums = [keep.tile([P, 4], F32, name=f"sums{i}") for i in range(PAIRS)]
+        denom = [keep.tile([P, 4], F32, name=f"denom{i}") for i in range(PAIRS)]
+        recip = [keep.tile([P, 4], F32, name=f"recip{i}") for i in range(PAIRS)]
+        ez = [keep.tile([P, R], F32, name=f"ez{b}") for b in range(BLOCKS)]
+        ey = [keep.tile([P, S], F32, name=f"ey{b}") for b in range(BLOCKS)]
+        py = [keep.tile([P, S], F32, name=f"py{b}") for b in range(BLOCKS)]
+        res = [keep.tile([P, S], F32, name=f"res{b}") for b in range(BLOCKS)]
+
+        def cast(b, engine):
+            raw = h_raw[b // 2][:, :, (b % 2) * P : (b % 2 + 1) * P]
+            dst = h_bf[b][:].rearrange("p (c i) j -> p c j i", i=4)
+            src = raw.rearrange("p j (c i) -> p c j i", i=4)
+            if engine == "scalar":
+                nc.scalar.copy(dst, src)
+            else:
+                nc.vector.tensor_copy(dst, src)
+
+        def quantize(b):
+            nc.vector.quantize_mx(
+                out=h_w[b][:].bitcast(FP8X4), scales=h_s[b][:], in_=h_bf[b][:].rearrange("p t j -> p (t j)")
+            )
+
+        def product(acc, b, words, scales):
+            nc.tensor.matmul_mx(
+                out=acc, lhsT=h_w[b][:].bitcast(FP8X4), lhsT_scale=h_s[b][:],
+                rhs=words[:].bitcast(FP8X4), rhs_scale=scales[:], start=True, stop=True,
+            )
+
+        def z_max(i):
+            nc.vector.tensor_reduce(z_negmax[i][:], z_ps[i][:], AXIS_X, ALU.max, negate=True)
+            nc.scalar.mul(z_bias[i][:], z_negmax[i][:], 0.7)
+
+        def z_exp(b):
+            i, u = divmod(b, 2)
+            nc.scalar.activation(
+                ez[b][:], z_ps[i][:, u, :], ACT.Exp, bias=z_bias[i][:, u : u + 1], scale=0.7,
+                accum_out=sums[i][:, u : u + 1],
+            )
+
+        def scatter(b):
+            nc.vector.tensor_copy(cp[b][:].indirect(word_t[:]), ez[b][:])
+
+        def y_max_exp(b):
+            i, u = divmod(b, 2)
+            nc.vector.tensor_reduce(y_negmax[b][:], y_ps[b][:], AXIS_X, ALU.max, negate=True)
+            nc.scalar.activation(
+                ey[b][:], y_ps[b][:], ACT.Exp, bias=y_negmax[b][:], accum_out=sums[i][:, 2 + u : 3 + u]
+            )
+
+        def normalisers(i):
+            nc.scalar.mul(denom[i][:, 0:2], sums[i][:, 0:2], 4.0)
+            nc.scalar.mul(denom[i][:, 2:4], sums[i][:, 2:4], 4.0 / 3.0)
+            nc.vector.reciprocal(recip[i][:], denom[i][:])
+            for u in range(2):
+                b = 2 * i + u
+                nc.scalar.activation(py[b][:], ey[b][:], ACT.Copy, scale=recip[i][:, 2 + u : 3 + u])
+
+        def mix_store(b):
+            i, u = divmod(b, 2)
+            nc.vector.scalar_tensor_tensor(
+                res[b][:], cp[b][:], recip[i][:, u : u + 1], py[b][:], ALU.mult, ALU.add
+            )
+            nc.sync.dma_start(out[b * P : (b + 1) * P, :], res[b][:])
+
+        def hidden(i):
+            for b in (2 * i, 2 * i + 1):
+                cast(b, "scalar")
+            for b in (2 * i, 2 * i + 1):
+                quantize(b)
+                product(z_ps[i][:, b % 2, :], b, eg_w, eg_s)
+
+        nc.vector.tensor_copy(eg_s[:], es[:].indirect(past_t[:]))
+        nc.vector.tensor_copy(eg_w[:], ew[:].bitcast(U32).indirect(past_t[:]))
+        nc.vector.tensor_copy(xg_s[:], xs[:].indirect(offs_t[:]))
+        hidden(0)
+        z_max(0)
+        z_exp(0)
+        z_exp(1)
+        nc.vector.tensor_copy(xg_w[:], xw[:].bitcast(U32).indirect(offs_t[:]))
+        product(y_ps[0][:], 0, xg_w, xg_s)
+        product(y_ps[1][:], 1, xg_w, xg_s)
+        hidden(1)
+        product(y_ps[2][:], 2, xg_w, xg_s)
+        product(y_ps[3][:], 3, xg_w, xg_s)
+        scatter(0)
+        y_max_exp(0)
+        y_max_exp(1)
+        scatter(1)
+        z_max(1)
+        z_exp(2)
+        z_exp(3)
+        normalisers(0)
+        y_max_exp(2)
+        y_max_exp(3)
+        mix_store(0)
+        mix_store(1)
+        scatter(2)
+        normalisers(1)
+        scatter(3)
+        mix_store(2)
+        mix_store(3)

@@ -31,7 +31,7 @@ def tile_picked_ycache_mix_p_kernel(tc, x_words, x_scales, hT, e_words, e_scales
         offs_t = keep.tile([P, S // 16], U16, name="offs_t")
         past_t = keep.tile([P, R // 16], U16, name="past_t")
         word_t = keep.tile([P, R // 16], U16, name="word_t")
-        xw = keep.tile([P, T], I32, name="xw")
+        xw = keep.tile([P, T], I32, name="xw", tag="x_table")
         ew = keep.tile([P, W], I32, name="ew")
         xs = keep.tile([P, T], U8, name="xs")
         es = keep.tile([P, W], U8, name="es")
@@ -40,7 +40,7 @@ def tile_picked_ycache_mix_p_kernel(tc, x_words, x_scales, hT, e_words, e_scales
         warm = keep.tile([P, 1], F32, name="warm")
         warm_out = keep.tile([P, 1], F32, name="warm_out")
 
-        nc.gpsimd.memset(es[:].bitcast(I32), 0)
+        nc.vector.memset(es[:].bitcast(I32), 0)
         nc.vector.memset(warm[:], 0.0)
         nc.vector.memset(xs[:].bitcast(I32), 0)
         nc.scalar.activation(warm_out[:], warm[:], ACT.Exp)
@@ -55,124 +55,143 @@ def tile_picked_ycache_mix_p_kernel(tc, x_words, x_scales, hT, e_words, e_scales
         h_view = hT.rearrange("(p j) t -> p j t", j=PACK)
         nc.sync.dma_start(past_t[:], past)
         nc.sync.dma_start(offs_t[:], offs)
-        nc.sync.dma_start(ew[:], e_words[0].rearrange("p n t -> p (n t)").bitcast(I32))
-        load_scales(es, e_scales)
         nc.sync.dma_start(h_raw[0][:], h_view[:, :, 0 : 2 * P])
+        load_scales(es, e_scales)
+        nc.sync.dma_start(ew[:], e_words[0].rearrange("p n t -> p (n t)").bitcast(I32))
+        nc.sync.dma_start(h_raw[1][:], h_view[:, :, 2 * P : 4 * P])
         load_scales(xs, x_scales)
         nc.sync.dma_start(xw[:], x_words[0].rearrange("p n t -> p (n t)").bitcast(I32))
-        nc.sync.dma_start(h_raw[1][:], h_view[:, :, 2 * P : 4 * P])
         nc.sync.dma_start(word_t[:], word)
 
         eg_w = keep.tile([P, R], U32, name="eg_w", align_bytes=64)
         eg_s = keep.tile([P, R], U8, name="eg_s", align_bytes=64)
         xg_w = keep.tile([P, S], U32, name="xg_w", align_bytes=64)
         xg_s = keep.tile([P, S], U8, name="xg_s", align_bytes=64)
-        h_bf = [keep.tile([P, P, PACK], BF16, name=f"h_bf{b}", align_bytes=64) for b in range(BLOCKS)]
-        h_w = [keep.tile([P, P], U32, name=f"h_w{b}", align_bytes=64) for b in range(BLOCKS)]
-        h_s = [keep.tile([P, P], U8, name=f"h_s{b}", align_bytes=64) for b in range(BLOCKS)]
+        h_bf = [keep.tile([P, 2 * P, PACK], BF16, name=f"h_bf{i}", align_bytes=64) for i in range(PAIRS)]
+        h_w = [keep.tile([P, 2 * P], U32, name=f"h_w{i}", align_bytes=64) for i in range(PAIRS)]
+        h_s = [keep.tile([P, 2 * P], U8, name=f"h_s{i}", align_bytes=64) for i in range(PAIRS)]
         z_ps = [psum.tile([P, 2, R], F32, name=f"z_ps{i}") for i in range(PAIRS)]
         y_ps = [psum.tile([P, S], F32, name=f"y_ps{b}") for b in range(BLOCKS)]
-        z_negmax = [keep.tile([P, 2], F32, name=f"z_negmax{i}") for i in range(PAIRS)]
+        after_x = keep.tile([P, 2 * R + 16], F32, name="after_x", tag="x_table")
+        z_negmax0 = keep.tile([P, 2], F32, name="z_negmax0")
+        z_negmax = [z_negmax0[:], after_x[:, 2 * R : 2 * R + 2]]
         z_bias = [keep.tile([P, 2], F32, name=f"z_bias{i}") for i in range(PAIRS)]
         y_negmax = [keep.tile([P, 1], F32, name=f"y_negmax{b}") for b in range(BLOCKS)]
-        sums = [keep.tile([P, 4], F32, name=f"sums{i}") for i in range(PAIRS)]
-        denom = [keep.tile([P, 4], F32, name=f"denom{i}") for i in range(PAIRS)]
-        recip = [keep.tile([P, 4], F32, name=f"recip{i}") for i in range(PAIRS)]
+        z_sum = [keep.tile([P, 2], F32, name=f"z_sum{i}") for i in range(PAIRS)]
+        y_sum = [keep.tile([P, 2], F32, name=f"y_sum{i}") for i in range(PAIRS)]
+        den_first = keep.tile([P, 2], F32, name="den_first")
+        den_mid = keep.tile([P, 4], F32, name="den_mid")
+        den_last = keep.tile([P, 2], F32, name="den_last")
+        rec_mid = keep.tile([P, 4], F32, name="rec_mid")
+        rec_last = keep.tile([P, 2], F32, name="rec_last")
+        rec_first = after_x[:, 2 * R + 8 : 2 * R + 10]
+        z_den = [den_first[:], den_mid[:, 2:4]]
+        y_den = [den_mid[:, 0:2], den_last[:]]
+        z_rec = [rec_first, rec_mid[:, 2:4]]
+        y_rec = [rec_mid[:, 0:2], rec_last[:]]
         ez = [keep.tile([P, R], F32, name=f"ez{b}") for b in range(BLOCKS)]
+        qz_late = keep.tile([P, 2 * R], F32, name="qz_late")
+        qz = [after_x[:, 0:R], after_x[:, R : 2 * R], qz_late[:, 0:R], qz_late[:, R : 2 * R]]
         ey = [keep.tile([P, S], F32, name=f"ey{b}") for b in range(BLOCKS)]
-        py = [keep.tile([P, S], F32, name=f"py{b}") for b in range(BLOCKS)]
         res = [keep.tile([P, S], F32, name=f"res{b}") for b in range(BLOCKS)]
 
         def cast(b, engine):
-            raw = h_raw[b // 2][:, :, (b % 2) * P : (b % 2 + 1) * P]
-            dst = h_bf[b][:].rearrange("p (c i) j -> p c j i", i=4)
-            src = raw.rearrange("p j (c i) -> p c j i", i=4)
+            i, u = divmod(b, 2)
+            dst = h_bf[i][:, u * P : (u + 1) * P, :].rearrange("p (c i) j -> p c j i", i=4)
+            src = h_raw[i][:, :, u * P : (u + 1) * P].rearrange("p j (c i) -> p c j i", i=4)
             if engine == "scalar":
                 nc.scalar.copy(dst, src)
             else:
                 nc.vector.tensor_copy(dst, src)
 
-        def quantize(b):
+        def hidden(i, second):
+            cast(2 * i, "scalar")
+            cast(2 * i + 1, second)
             nc.vector.quantize_mx(
-                out=h_w[b][:].bitcast(FP8X4), scales=h_s[b][:], in_=h_bf[b][:].rearrange("p t j -> p (t j)")
+                out=h_w[i][:].bitcast(FP8X4), scales=h_s[i][:], in_=h_bf[i][:].rearrange("p t j -> p (t j)")
             )
 
         def product(acc, b, words, scales):
+            i, u = divmod(b, 2)
+            cols = slice(u * P, (u + 1) * P)
             nc.tensor.matmul_mx(
-                out=acc, lhsT=h_w[b][:].bitcast(FP8X4), lhsT_scale=h_s[b][:],
+                out=acc, lhsT=h_w[i][:, cols].bitcast(FP8X4), lhsT_scale=h_s[i][:, cols],
                 rhs=words[:].bitcast(FP8X4), rhs_scale=scales[:], start=True, stop=True,
             )
 
-        def z_max(i):
-            nc.vector.tensor_reduce(z_negmax[i][:], z_ps[i][:], AXIS_X, ALU.max, negate=True)
-            nc.scalar.mul(z_bias[i][:], z_negmax[i][:], 0.7)
+        def z_products(i):
+            for u in range(2):
+                product(z_ps[i][:, u, :], 2 * i + u, eg_w, eg_s)
 
-        def z_exp(b):
+        def z_max(i):
+            nc.vector.tensor_reduce(z_negmax[i], z_ps[i][:], AXIS_X, ALU.max, negate=True)
+            nc.scalar.mul(z_bias[i][:], z_negmax[i], 0.7)
+
+        def z_exp(i):
+            for u in range(2):
+                nc.scalar.activation(
+                    ez[2 * i + u][:], z_ps[i][:, u, :], ACT.Exp, bias=z_bias[i][:, u : u + 1], scale=0.7,
+                    accum_out=z_sum[i][:, u : u + 1],
+                )
+            nc.scalar.mul(z_den[i], z_sum[i][:], 4.0)
+
+        def z_scale(b):
             i, u = divmod(b, 2)
-            nc.scalar.activation(
-                ez[b][:], z_ps[i][:, u, :], ACT.Exp, bias=z_bias[i][:, u : u + 1], scale=0.7,
-                accum_out=sums[i][:, u : u + 1],
-            )
+            nc.scalar.activation(qz[b], ez[b][:], ACT.Copy, scale=z_rec[i][:, u : u + 1])
 
         def scatter(b):
-            nc.vector.tensor_copy(cp[b][:].indirect(word_t[:]), ez[b][:])
+            nc.vector.tensor_copy(cp[b][:].indirect(word_t[:]), qz[b])
 
         def y_max_exp(b):
             i, u = divmod(b, 2)
             nc.vector.tensor_reduce(y_negmax[b][:], y_ps[b][:], AXIS_X, ALU.max, negate=True)
             nc.scalar.activation(
-                ey[b][:], y_ps[b][:], ACT.Exp, bias=y_negmax[b][:], accum_out=sums[i][:, 2 + u : 3 + u]
+                ey[b][:], y_ps[b][:], ACT.Exp, bias=y_negmax[b][:], accum_out=y_sum[i][:, u : u + 1]
             )
 
-        def normalisers(i):
-            nc.scalar.mul(denom[i][:, 0:2], sums[i][:, 0:2], 4.0)
-            nc.scalar.mul(denom[i][:, 2:4], sums[i][:, 2:4], 4.0 / 3.0)
-            nc.vector.reciprocal(recip[i][:], denom[i][:])
-            for u in range(2):
-                b = 2 * i + u
-                nc.scalar.activation(py[b][:], ey[b][:], ACT.Copy, scale=recip[i][:, 2 + u : 3 + u])
+        def y_denominators(i):
+            nc.scalar.mul(y_den[i], y_sum[i][:], 4.0 / 3.0)
 
-        def mix_store(b):
+        def mix_store(b, cols):
             i, u = divmod(b, 2)
             nc.vector.scalar_tensor_tensor(
-                res[b][:], cp[b][:], recip[i][:, u : u + 1], py[b][:], ALU.mult, ALU.add
+                res[b][:, cols], ey[b][:, cols], y_rec[i][:, u : u + 1], cp[b][:, cols], ALU.mult, ALU.add
             )
-            nc.sync.dma_start(out[b * P : (b + 1) * P, :], res[b][:])
-
-        def hidden(i):
-            for b in (2 * i, 2 * i + 1):
-                cast(b, "scalar")
-            for b in (2 * i, 2 * i + 1):
-                quantize(b)
-                product(z_ps[i][:, b % 2, :], b, eg_w, eg_s)
+            nc.sync.dma_start(out[b * P : (b + 1) * P, cols], res[b][:, cols])
 
         nc.vector.tensor_copy(eg_s[:], es[:].indirect(past_t[:]))
+        hidden(0, "vector")
         nc.vector.tensor_copy(eg_w[:], ew[:].bitcast(U32).indirect(past_t[:]))
-        nc.vector.tensor_copy(xg_s[:], xs[:].indirect(offs_t[:]))
-        hidden(0)
+        z_products(0)
         z_max(0)
+        nc.vector.tensor_copy(xg_s[:], xs[:].indirect(offs_t[:]))
+        hidden(1, "vector")
+        z_products(1)
         z_exp(0)
-        z_exp(1)
         nc.vector.tensor_copy(xg_w[:], xw[:].bitcast(U32).indirect(offs_t[:]))
-        product(y_ps[0][:], 0, xg_w, xg_s)
-        product(y_ps[1][:], 1, xg_w, xg_s)
-        hidden(1)
-        product(y_ps[2][:], 2, xg_w, xg_s)
-        product(y_ps[3][:], 3, xg_w, xg_s)
+        for b in range(BLOCKS):
+            product(y_ps[b][:], b, xg_w, xg_s)
+        nc.vector.reciprocal(rec_first, den_first[:])
+        z_max(1)
+        z_scale(0)
+        z_scale(1)
+        z_exp(1)
         scatter(0)
+        scatter(1)
         y_max_exp(0)
         y_max_exp(1)
-        scatter(1)
-        z_max(1)
-        z_exp(2)
-        z_exp(3)
-        normalisers(0)
+        y_denominators(0)
+        nc.vector.reciprocal(rec_mid[:], den_mid[:])
+        z_scale(2)
+        z_scale(3)
         y_max_exp(2)
         y_max_exp(3)
-        mix_store(0)
-        mix_store(1)
+        y_denominators(1)
+        mix_store(0, slice(0, S))
+        mix_store(1, slice(0, S))
         scatter(2)
-        normalisers(1)
+        nc.vector.reciprocal(rec_last[:], den_last[:])
         scatter(3)
-        mix_store(2)
-        mix_store(3)
+        mix_store(2, slice(0, S))
+        mix_store(3, slice(0, S // 2))
+        mix_store(3, slice(S // 2, S))

@@ -37,14 +37,12 @@ def tile_picked_ycache_mix_p_kernel(tc, x_words, x_scales, hT, e_words, e_scales
         es = keep.tile([P, W], U8, name="es")
         h_raw = [keep.tile([P, PACK, 2 * P], F32, name=f"h_raw{i}") for i in range(PAIRS)]
         cp = [keep.tile([P, S], F32, name=f"cp{b}") for b in range(BLOCKS)]
-        warm = keep.tile([P, 1], F32, name="warm")
-        warm_out = keep.tile([P, 1], F32, name="warm_out")
 
         nc.vector.memset(es[:].bitcast(I32), 0)
-        nc.vector.memset(warm[:], 0.0)
         nc.vector.memset(xs[:].bitcast(I32), 0)
-        nc.scalar.activation(warm_out[:], warm[:], ACT.Exp)
-        for b in range(BLOCKS):
+        nc.gpsimd.memset(cp[0][:], 0.0)
+        nc.scalar.copy(cp[1][:], cp[0][:])
+        for b in range(2, BLOCKS):
             nc.vector.memset(cp[b][:], 0.0)
 
         def load_scales(tile, scales):
@@ -65,16 +63,17 @@ def tile_picked_ycache_mix_p_kernel(tc, x_words, x_scales, hT, e_words, e_scales
 
         eg_w = keep.tile([P, R], U32, name="eg_w", align_bytes=64)
         eg_s = keep.tile([P, R], U8, name="eg_s", align_bytes=64)
-        xg_w = keep.tile([P, S], U32, name="xg_w", align_bytes=64)
+        xg_w = keep.tile([P, S], U32, name="xg_w", tag="x_picked", align_bytes=64)
         xg_s = keep.tile([P, S], U8, name="xg_s", align_bytes=64)
         h_bf = [keep.tile([P, 2 * P, PACK], BF16, name=f"h_bf{i}", align_bytes=64) for i in range(PAIRS)]
         h_w = [keep.tile([P, 2 * P], U32, name=f"h_w{i}", align_bytes=64) for i in range(PAIRS)]
         h_s = [keep.tile([P, 2 * P], U8, name=f"h_s{i}", align_bytes=64) for i in range(PAIRS)]
         z_ps = [psum.tile([P, 2, R], F32, name=f"z_ps{i}") for i in range(PAIRS)]
         y_ps = [psum.tile([P, S], F32, name=f"y_ps{b}") for b in range(BLOCKS)]
-        after_x = keep.tile([P, 2 * R + 16], F32, name="after_x", tag="x_table")
+        after_x = keep.tile([P, 16], F32, name="after_x", tag="x_table")
+        qz_early = keep.tile([P, 2 * R], F32, name="qz_early", tag="x_picked", align_bytes=64)
         z_negmax0 = keep.tile([P, 2], F32, name="z_negmax0")
-        z_negmax = [z_negmax0[:], after_x[:, 2 * R : 2 * R + 2]]
+        z_negmax = [z_negmax0[:], after_x[:, 0:2]]
         z_bias = [keep.tile([P, 2], F32, name=f"z_bias{i}") for i in range(PAIRS)]
         y_negmax = [keep.tile([P, 1], F32, name=f"y_negmax{b}") for b in range(BLOCKS)]
         z_sum = [keep.tile([P, 2], F32, name=f"z_sum{i}") for i in range(PAIRS)]
@@ -84,15 +83,16 @@ def tile_picked_ycache_mix_p_kernel(tc, x_words, x_scales, hT, e_words, e_scales
         den_last = keep.tile([P, 2], F32, name="den_last")
         rec_mid = keep.tile([P, 4], F32, name="rec_mid")
         rec_last = keep.tile([P, 2], F32, name="rec_last")
-        rec_first = after_x[:, 2 * R + 8 : 2 * R + 10]
+        rec_first = after_x[:, 8:10]
         z_den = [den_first[:], den_mid[:, 2:4]]
         y_den = [den_mid[:, 0:2], den_last[:]]
         z_rec = [rec_first, rec_mid[:, 2:4]]
         y_rec = [rec_mid[:, 0:2], rec_last[:]]
         ez = [keep.tile([P, R], F32, name=f"ez{b}") for b in range(BLOCKS)]
         qz_late = keep.tile([P, 2 * R], F32, name="qz_late")
-        qz = [after_x[:, 0:R], after_x[:, R : 2 * R], qz_late[:, 0:R], qz_late[:, R : 2 * R]]
+        qz = [qz_early[:, 0:R], qz_early[:, R : 2 * R], qz_late[:, 0:R], qz_late[:, R : 2 * R]]
         ey = [keep.tile([P, S], F32, name=f"ey{b}") for b in range(BLOCKS)]
+        py = [keep.tile([P, S], F32, name=f"py{b}") for b in range(BLOCKS)]
         res = [keep.tile([P, S], F32, name=f"res{b}") for b in range(BLOCKS)]
 
         def cast(b, engine):
@@ -159,6 +159,14 @@ def tile_picked_ycache_mix_p_kernel(tc, x_words, x_scales, hT, e_words, e_scales
             )
             nc.sync.dma_start(out[b * P : (b + 1) * P, cols], res[b][:, cols])
 
+        def y_scale(b, cols):
+            i, u = divmod(b, 2)
+            nc.scalar.activation(py[b][:, cols], ey[b][:, cols], ACT.Copy, scale=y_rec[i][:, u : u + 1])
+
+        def add_store(b, cols):
+            nc.gpsimd.tensor_tensor(res[b][:, cols], py[b][:, cols], cp[b][:, cols], ALU.add)
+            nc.sync.dma_start(out[b * P : (b + 1) * P, cols], res[b][:, cols])
+
         nc.vector.tensor_copy(eg_s[:], es[:].indirect(past_t[:]))
         hidden(0, "vector")
         nc.vector.tensor_copy(eg_w[:], ew[:].bitcast(U32).indirect(past_t[:]))
@@ -173,25 +181,29 @@ def tile_picked_ycache_mix_p_kernel(tc, x_words, x_scales, hT, e_words, e_scales
             product(y_ps[b][:], b, xg_w, xg_s)
         nc.vector.reciprocal(rec_first, den_first[:])
         z_max(1)
-        z_scale(0)
-        z_scale(1)
         z_exp(1)
-        scatter(0)
-        scatter(1)
         y_max_exp(0)
+        z_scale(0)
         y_max_exp(1)
         y_denominators(0)
-        nc.vector.reciprocal(rec_mid[:], den_mid[:])
-        z_scale(2)
-        z_scale(3)
+        z_scale(1)
         y_max_exp(2)
         y_max_exp(3)
         y_denominators(1)
-        mix_store(0, slice(0, S))
-        mix_store(1, slice(0, S))
-        scatter(2)
+        scatter(0)
+        nc.vector.reciprocal(rec_mid[:], den_mid[:])
+        scatter(1)
         nc.vector.reciprocal(rec_last[:], den_last[:])
+        z_scale(2)
+        y_scale(0, slice(0, S))
+        add_store(0, slice(0, S))
+        z_scale(3)
+        y_scale(1, slice(0, S))
+        add_store(1, slice(0, S))
+        scatter(2)
+        y_scale(2, slice(0, S // 2))
+        add_store(2, slice(0, S // 2))
         scatter(3)
-        mix_store(2, slice(0, S))
+        mix_store(2, slice(S // 2, S))
         mix_store(3, slice(0, S // 2))
         mix_store(3, slice(S // 2, S))

from contextlib import ExitStack

import concourse.mybir as mybir

K, T, S, V, R, W = 512, 2048, 512, 512, 256, 1024
FLOPS = 2 * K * V * (S + R)

F32 = mybir.dt.float32
BF16 = mybir.dt.bfloat16
I32 = mybir.dt.int32
U32 = mybir.dt.uint32
U16 = mybir.dt.uint16
U8 = mybir.dt.uint8
FP8X4 = mybir.dt.float8_e4m3fn_x4
ALU = mybir.AluOpType
ACT = mybir.ActivationFunctionType
AXIS_X = mybir.AxisListType.X

P = 128
PACK = 4
BLOCKS = V // P
PAIRS = BLOCKS // 2


def tile_picked_ycache_mix_p_kernel(tc, x_words, x_scales, hT, e_words, e_scales, offs, past, word, out):
    nc = tc.nc
    with ExitStack() as ctx:
        keep = ctx.enter_context(tc.tile_pool(name="keep", bufs=1))
        psum = ctx.enter_context(tc.psum_pool(name="psum", bufs=1))

        offs_t = keep.tile([P, S // 16], U16, name="offs_t")
        past_t = keep.tile([P, R // 16], U16, name="past_t")
        word_t = keep.tile([P, R // 16], U16, name="word_t")
        xw = keep.tile([P, T], I32, name="xw", tag="x_table")
        ew = keep.tile([P, W], I32, name="ew")
        xs = keep.tile([P, T], U8, name="xs")
        es = keep.tile([P, W], U8, name="es")
        h_raw = [keep.tile([P, PACK, 2 * P], F32, name=f"h_raw{i}") for i in range(PAIRS)]
        cp = [keep.tile([P, S], F32, name=f"cp{b}") for b in range(BLOCKS)]

        nc.vector.memset(es[:].bitcast(I32), 0)
        nc.vector.memset(xs[:].bitcast(I32), 0)
        nc.gpsimd.memset(cp[0][:], 0.0)
        nc.scalar.copy(cp[1][:], cp[0][:])
        for b in range(2, BLOCKS):
            nc.vector.memset(cp[b][:], 0.0)

        def load_scales(tile, scales):
            rows = scales[0].rearrange("(q r) n -> r q n", r=4)
            for r in range(4):
                nc.sync.dma_start(tile[r:P:32, :].bitcast(I32), rows[r].bitcast(I32))

        h_view = hT.rearrange("(p j) t -> p j t", j=PACK)
        nc.sync.dma_start(past_t[:], past)
        nc.sync.dma_start(offs_t[:], offs)
        nc.sync.dma_start(h_raw[0][:], h_view[:, :, 0 : 2 * P])
        load_scales(es, e_scales)
        nc.sync.dma_start(ew[:], e_words[0].rearrange("p n t -> p (n t)").bitcast(I32))
        nc.sync.dma_start(h_raw[1][:], h_view[:, :, 2 * P : 4 * P])
        load_scales(xs, x_scales)
        nc.sync.dma_start(xw[:], x_words[0].rearrange("p n t -> p (n t)").bitcast(I32))
        nc.sync.dma_start(word_t[:], word)

        eg_w = keep.tile([P, R], U32, name="eg_w", align_bytes=64)
        eg_s = keep.tile([P, R], U8, name="eg_s", align_bytes=64)
        xg_w = keep.tile([P, S], U32, name="xg_w", tag="x_picked", align_bytes=64)
        xg_s = keep.tile([P, S], U8, name="xg_s", align_bytes=64)
        h_bf = [keep.tile([P, 2 * P, PACK], BF16, name=f"h_bf{i}", align_bytes=64) for i in range(PAIRS)]
        h_w = [keep.tile([P, 2 * P], U32, name=f"h_w{i}", align_bytes=64) for i in range(PAIRS)]
        h_s = [keep.tile([P, 2 * P], U8, name=f"h_s{i}", align_bytes=64) for i in range(PAIRS)]
        z_ps = [psum.tile([P, 2, R], F32, name=f"z_ps{i}") for i in range(PAIRS)]
        y_ps = [psum.tile([P, S], F32, name=f"y_ps{b}") for b in range(BLOCKS)]
        after_x = keep.tile([P, 16], F32, name="after_x", tag="x_table")
        qz_early = keep.tile([P, 2 * R], F32, name="qz_early", tag="x_picked", align_bytes=64)
        z_negmax0 = keep.tile([P, 2], F32, name="z_negmax0")
        z_negmax = [z_negmax0[:], after_x[:, 0:2]]
        z_bias = [keep.tile([P, 2], F32, name=f"z_bias{i}") for i in range(PAIRS)]
        y_negmax = [keep.tile([P, 1], F32, name=f"y_negmax{b}") for b in range(BLOCKS)]
        z_sum = [keep.tile([P, 2], F32, name=f"z_sum{i}") for i in range(PAIRS)]
        y_sum = [keep.tile([P, 2], F32, name=f"y_sum{i}") for i in range(PAIRS)]
        den_first = keep.tile([P, 2], F32, name="den_first")
        den_mid = keep.tile([P, 4], F32, name="den_mid")
        den_last = keep.tile([P, 2], F32, name="den_last")
        rec_mid = keep.tile([P, 4], F32, name="rec_mid")
        rec_last = keep.tile([P, 2], F32, name="rec_last")
        rec_first = after_x[:, 8:10]
        z_den = [den_first[:], den_mid[:, 2:4]]
        y_den = [den_mid[:, 0:2], den_last[:]]
        z_rec = [rec_first, rec_mid[:, 2:4]]
        y_rec = [rec_mid[:, 0:2], rec_last[:]]
        ez = [keep.tile([P, R], F32, name=f"ez{b}") for b in range(BLOCKS)]
        qz_late = keep.tile([P, 2 * R], F32, name="qz_late")
        qz = [qz_early[:, 0:R], qz_early[:, R : 2 * R], qz_late[:, 0:R], qz_late[:, R : 2 * R]]
        ey = [keep.tile([P, S], F32, name=f"ey{b}") for b in range(BLOCKS)]
        py = [keep.tile([P, S], F32, name=f"py{b}") for b in range(BLOCKS)]
        res = [keep.tile([P, S], F32, name=f"res{b}") for b in range(BLOCKS)]

        def cast(b, engine):
            i, u = divmod(b, 2)
            dst = h_bf[i][:, u * P : (u + 1) * P, :].rearrange("p (c i) j -> p c j i", i=4)
            src = h_raw[i][:, :, u * P : (u + 1) * P].rearrange("p j (c i) -> p c j i", i=4)
            if engine == "scalar":
                nc.scalar.copy(dst, src)
            else:
                nc.vector.tensor_copy(dst, src)

        def hidden(i, second):
            cast(2 * i, "scalar")
            cast(2 * i + 1, second)
            nc.vector.quantize_mx(
                out=h_w[i][:].bitcast(FP8X4), scales=h_s[i][:], in_=h_bf[i][:].rearrange("p t j -> p (t j)")
            )

        def product(acc, b, words, scales):
            i, u = divmod(b, 2)
            cols = slice(u * P, (u + 1) * P)
            nc.tensor.matmul_mx(
                out=acc, lhsT=h_w[i][:, cols].bitcast(FP8X4), lhsT_scale=h_s[i][:, cols],
                rhs=words[:].bitcast(FP8X4), rhs_scale=scales[:], start=True, stop=True,
            )

        def z_products(i):
            for u in range(2):
                product(z_ps[i][:, u, :], 2 * i + u, eg_w, eg_s)

        def z_max(i):
            nc.vector.tensor_reduce(z_negmax[i], z_ps[i][:], AXIS_X, ALU.max, negate=True)
            nc.scalar.mul(z_bias[i][:], z_negmax[i], 0.7)

        def z_exp(i):
            for u in range(2):
                nc.scalar.activation(
                    ez[2 * i + u][:], z_ps[i][:, u, :], ACT.Exp, bias=z_bias[i][:, u : u + 1], scale=0.7,
                    accum_out=z_sum[i][:, u : u + 1],
                )
            nc.scalar.mul(z_den[i], z_sum[i][:], 4.0)

        def z_scale(b):
            i, u = divmod(b, 2)
            nc.scalar.activation(qz[b], ez[b][:], ACT.Copy, scale=z_rec[i][:, u : u + 1])

        def scatter(b):
            nc.vector.tensor_copy(cp[b][:].indirect(word_t[:]), qz[b])

        def y_max_exp(b):
            i, u = divmod(b, 2)
            nc.vector.tensor_reduce(y_negmax[b][:], y_ps[b][:], AXIS_X, ALU.max, negate=True)
            nc.scalar.activation(
                ey[b][:], y_ps[b][:], ACT.Exp, bias=y_negmax[b][:], accum_out=y_sum[i][:, u : u + 1]
            )

        def y_denominators(i):
            nc.scalar.mul(y_den[i], y_sum[i][:], 4.0 / 3.0)

        def mix_store(b, cols):
            i, u = divmod(b, 2)
            nc.vector.scalar_tensor_tensor(
                res[b][:, cols], ey[b][:, cols], y_rec[i][:, u : u + 1], cp[b][:, cols], ALU.mult, ALU.add
            )
            nc.sync.dma_start(out[b * P : (b + 1) * P, cols], res[b][:, cols])

        def y_scale(b, cols):
            i, u = divmod(b, 2)
            nc.scalar.activation(py[b][:, cols], ey[b][:, cols], ACT.Copy, scale=y_rec[i][:, u : u + 1])

        def add_store(b, cols):
            nc.gpsimd.tensor_tensor(res[b][:, cols], py[b][:, cols], cp[b][:, cols], ALU.add)
            nc.sync.dma_start(out[b * P : (b + 1) * P, cols], res[b][:, cols])

        nc.vector.tensor_copy(eg_s[:], es[:].indirect(past_t[:]))
        hidden(0, "vector")
        nc.vector.tensor_copy(eg_w[:], ew[:].bitcast(U32).indirect(past_t[:]))
        z_products(0)
        z_max(0)
        nc.vector.tensor_copy(xg_s[:], xs[:].indirect(offs_t[:]))
        hidden(1, "vector")
        z_products(1)
        z_exp(0)
        nc.vector.tensor_copy(xg_w[:], xw[:].bitcast(U32).indirect(offs_t[:]))
        for b in range(BLOCKS):
            product(y_ps[b][:], b, xg_w, xg_s)
        nc.vector.reciprocal(rec_first, den_first[:])
        z_max(1)
        z_exp(1)
        y_max_exp(0)
        z_scale(0)
        y_max_exp(1)
        y_denominators(0)
        z_scale(1)
        y_max_exp(2)
        y_max_exp(3)
        y_denominators(1)
        scatter(0)
        nc.vector.reciprocal(rec_mid[:], den_mid[:])
        scatter(1)
        nc.vector.reciprocal(rec_last[:], den_last[:])
        z_scale(2)
        y_scale(0, slice(0, S))
        add_store(0, slice(0, S))
        z_scale(3)
        y_scale(1, slice(0, S))
        add_store(1, slice(0, S))
        scatter(2)
        y_scale(2, slice(0, S // 2))
        add_store(2, slice(0, S // 2))
        scatter(3)
        mix_store(2, slice(S // 2, S))
        mix_store(3, slice(0, S // 2))
        mix_store(3, slice(S // 2, S))
